import numpy as np
import ml_dtypes


def mxq(x, axis, fmt="e4m3"):
    dtype, down = {"e4m3": (ml_dtypes.float8_e4m3fn, 7), "e5m2": (ml_dtypes.float8_e5m2, 14)}[fmt]
    v = np.moveaxis(np.asarray(x, np.float32).astype(ml_dtypes.bfloat16).astype(np.float64), axis, -1)
    blocks = v.reshape(v.shape[:-1] + (-1, 32))
    amax = np.abs(blocks).max(-1, keepdims=True)
    byte = np.maximum(np.where(amax > 0, np.frexp(amax)[1] - 1 + 127, 0) - down, 1)
    scale = np.exp2(byte - 127.0)
    codes = (blocks / scale).astype(np.float32).astype(dtype).astype(np.float64)
    return np.moveaxis((codes * scale).reshape(v.shape), -1, axis)


WIDE = False


def mx_kscale(k):
    if not WIDE:
        return np.ones(k)
    levels = np.array([10, -10, 5, -5, 0])
    if k % 512:
        return np.exp2(np.random.permutation(np.resize(levels, k // 32))).repeat(32)
    a = np.empty((k // 512, 16))
    for p in range(k // 512):
        a[p, :8] = np.random.permutation(np.resize(levels, 8))
        for g in range(8):
            far = levels[np.abs(levels - a[p, g]) >= 10]
            a[p, g + 8] = far[np.random.randint(len(far))]
    return np.exp2(a.ravel()).repeat(32)


def f64(x):
    return np.asarray(x).astype(np.float64)


def striped(idx):
    return np.tile(idx.reshape(-1, 16).T, (8, 1)).astype(np.uint16)


def unstriped(offs):
    return offs[:16].T.reshape(-1).astype(np.int64)


def striped8(idx):
    return np.concatenate([x.reshape(-1, 16).T for x in idx]).astype(np.uint16)


def runs(offs, k):
    lists = np.stack([offs[16 * r : 16 * r + 16].T.reshape(-1) for r in range(8)]).astype(np.int64)
    return lists[np.arange(k) % 512 // 64]


def pack_weight(w):
    k, n = w.shape
    w = f64(np.asarray(w, np.float32).astype(ml_dtypes.bfloat16)).reshape(k // 32, 32, n)
    amax = np.abs(w).max(1)
    byte = np.clip(np.where(amax > 0, np.frexp(amax)[1] - 1 + 127 - 7, 1), 1, 254)
    scaled = (w * np.exp2(127.0 - byte)[:, None, :]).reshape(k, n).astype(np.float32)
    words = np.ascontiguousarray(scaled.reshape(k // 512, 128, 4, n).transpose(0, 1, 3, 2)).astype(ml_dtypes.float8_e4m3fn).view(np.uint8)
    return words, np.ascontiguousarray(byte.astype(np.uint8).reshape(k // 512, 16, n))


def unpack_weight(words, scales):
    g, p, n, _ = words.shape
    vals = np.ascontiguousarray(words).view(ml_dtypes.float8_e4m3fn).astype(np.float64) * np.repeat(np.exp2(scales.astype(np.float64) - 127.0), 8, axis=1)[..., None]
    return vals.transpose(0, 1, 3, 2).reshape(g * 512, n)


def sigmoid(v):
    return 1.0 / (1.0 + np.exp(-np.maximum(v, -700.0)))


K, T, S, N, G, H, W = 512, 1024, 256, 512, 2048, 512, 128


def setup_inputs():
    n = np.random.standard_normal
    s = mx_kscale(K)[:, None]
    u = mx_kscale(K)
    packed_xT = pack_weight(n((K, T)) * s)
    packed_dT = pack_weight(n((K, G)) / s)
    perm = np.random.permutation(S)
    return {
        "x_words": packed_xT[0],
        "x_scales": packed_xT[1],
        "d_words": packed_dT[0],
        "d_scales": packed_dT[1],
        "gn": (np.random.uniform(0.5, 1.5, (H, 1)) * u[:, None]).astype(np.float32),
        "w1": (n((H, N)) / np.sqrt(2 * H) / u[:, None]).astype(np.float32),
        "w2": (n((K, N)) / np.sqrt(2 * K) / s).astype(np.float32),
        "offs": striped(np.random.permutation(T)[:S]),
        "k1": striped8(np.random.randint(0, G, (8, H))),
        "n1": striped(perm[:W]),
        "n2": striped(perm[W:]),
        "two": striped(np.random.permutation(T)[:S]),
        "n3": striped8(np.stack([np.random.permutation(S) for _ in range(8)])),
        "n4": striped8(np.stack([np.random.permutation(S) for _ in range(8)])),
    }


def reference(x_words, x_scales, d_words, d_scales, gn, w1, w2, offs, k1, n1, n2, two, n3, n4):
    d_k1 = unpack_weight(d_words, d_scales)[np.arange(K)[:, None], runs(k1, K)]
    xq = unpack_weight(x_words, x_scales)[:, unstriped(offs)]
    h = 0.0625 * (d_k1.T @ xq)
    pa = h[:, unstriped(n1)]
    pb = h[:, unstriped(n2)]
    ra = np.maximum(pa, pb)
    ds = h.copy()
    ds[:, unstriped(n1)] = ra
    z = f64(gn) * ds
    x_two = unpack_weight(x_words, x_scales)[:, unstriped(two)]
    h2 = mxq(f64(w1), 0, "e4m3").T @ mxq(z, 0, "e4m3") + mxq(f64(w2), 0, "e4m3").T @ x_two
    st = h2[np.arange(N)[:, None], runs(n3, N)] - h2
    return h2 * (sigmoid(st[np.arange(N)[:, None], runs(n4, N)]))

@@ -1,0 +1,172 @@
+from contextlib import ExitStack
+
+import concourse.mybir as mybir
+
+K, T, S, N, G, H, W = 512, 1024, 256, 512, 2048, 512, 128
+FLOPS = 2 * K * H * S + 2 * H * N * S + 2 * K * N * S
+
+F32 = mybir.dt.float32
+BF16 = mybir.dt.bfloat16
+I32 = mybir.dt.int32
+U32 = mybir.dt.uint32
+U16 = mybir.dt.uint16
+U8 = mybir.dt.uint8
+FP8X4 = mybir.dt.float8_e4m3fn_x4
+ALU = mybir.AluOpType
+ACT = mybir.ActivationFunctionType
+
+P = 128
+PACK = 4
+N2_ENG = ["s","s","s","s"]
+EVAC = ["s","s","s","s"]
+EVAC2 = ["v","v","v","v"]
+CAST_PARTS = 1
+
+
+def tile_picked_pqmixfillhopd_none_p_kernel(tc, x_words, x_scales, d_words, d_scales, gn, w1, w2, offs, k1, n1, n2, two, n3, n4, out):
+    nc = tc.nc
+    with ExitStack() as ctx:
+        sb = ctx.enter_context(tc.tile_pool(name="sb", bufs=1))
+        reuse = ctx.enter_context(tc.tile_pool(name="reuse", bufs=1))
+        psum = ctx.enter_context(tc.psum_pool(name="psum", bufs=1))
+
+        def load_list(name, src):
+            lst = sb.tile(list(src.shape), U16, name=name)
+            nc.sync.dma_start(lst[:], src)
+            return lst
+
+        def load_scale_rows(queue, table, scales):
+            rows = scales[0].bitcast(I32).rearrange("(r c) n -> c r n", c=2)
+            for c in range(2):
+                queue.dma_start(table[c:P:16, :].bitcast(I32), rows[c])
+
+        def place_odd_rows(plane):
+            for c in range(2):
+                nc.sync.dma_start(plane[2 + c : P : 32, :].bitcast(I32), plane[16 + c : P : 32, :].bitcast(I32))
+
+        d_byte_table = sb.tile([P, G], U8, name="d_byte_table")
+        x_byte_table = sb.tile([P, T], U8, name="x_byte_table")
+        nc.vector.memset(d_byte_table[:].bitcast(I32), 0)
+        nc.gpsimd.memset(x_byte_table[:].bitcast(I32), 0)
+
+        k1_t = load_list("k1_t", k1)
+        offs_t = load_list("offs_t", offs)
+        two_t = load_list("two_t", two)
+        load_scale_rows(nc.sync, d_byte_table, d_scales)
+        load_scale_rows(nc.scalar, x_byte_table, x_scales)
+        d_word_table = sb.tile([P, G], U32, name="d_word_table")
+        nc.sync.dma_start(d_word_table[:].bitcast(I32), d_words[0].rearrange("p n t -> p (n t)").bitcast(I32))
+        x_word_table = sb.tile([P, T], U32, name="x_word_table")
+        nc.sync.dma_start(x_word_table[:].bitcast(I32), x_words[0].rearrange("p n t -> p (n t)").bitcast(I32))
+        n1_t = load_list("n1_t", n1)
+        n2_t = load_list("n2_t", n2)
+        gain = sb.tile([P, PACK], F32, name="gain")
+        nc.gpsimd.dma_start(gain[:], gn.rearrange("(p t) o -> p (t o)", t=PACK))
+        n3_t = load_list("n3_t", n3)
+        n4_t = load_list("n4_t", n4)
+
+        raw_bytes = PACK * N * 4
+        d_bytes_picked = sb.tile([P, H], U8, name="d_bytes_picked", tag="bytes_picked")
+        nc.vector.tensor_copy(d_bytes_picked[:], d_byte_table[:].indirect(k1_t[:]))
+        xq_bytes_picked = reuse.tile([P, S], U8, name="xq_bytes_picked", offset=raw_bytes - S // 2)
+        nc.vector.tensor_copy(xq_bytes_picked[:], x_byte_table[:].indirect(offs_t[:]))
+        plane = sb.tile([P, H + S], U8, name="plane", align_bytes=64)
+        nc.vector.tensor_copy(plane[:, :H].rearrange("p (t m) -> p m t", t=PACK), d_bytes_picked[:].rearrange("p (m t) -> p m t", t=PACK))
+        nc.vector.tensor_copy(plane[:, H:].bitcast(I32), xq_bytes_picked[:].bitcast(I32))
+        place_odd_rows(plane)
+        w2_raw = reuse.tile([P, PACK, N], F32, name="w2_raw", offset=0)
+        nc.sync.dma_start(w2_raw[:], w2.rearrange("(p j) c -> p j c", j=PACK))
+        w1_raw = reuse.tile([P, PACK, N], F32, name="w1_raw", offset=raw_bytes)
+        nc.sync.dma_start(w1_raw[:], w1.rearrange("(p j) c -> p j c", j=PACK))
+
+        d_words_picked = sb.tile([P, H], U32, name="d_words_picked")
+        nc.vector.tensor_copy(d_words_picked[:], d_word_table[:].indirect(k1_t[:]))
+        d_codes = sb.tile([P, PACK, P], U32, name="d_codes", align_bytes=64)
+        nc.vector.tensor_copy(d_codes[:].bitcast(I32).rearrange("p t m -> p m t"), d_words_picked[:].bitcast(I32).rearrange("p (m t) -> p m t", t=PACK))
+        xq_codes = sb.tile([P, S], U32, name="xq_codes", align_bytes=64)
+        nc.vector.tensor_copy(xq_codes[:], x_word_table[:].indirect(offs_t[:]))
+
+        x2_bytes_picked = sb.tile([P, S], U8, name="x2_bytes_picked", tag="bytes_picked")
+        nc.vector.tensor_copy(x2_bytes_picked[:], x_byte_table[:].indirect(two_t[:]))
+        x2_bytes = sb.tile([P, S], U8, name="x2_bytes", align_bytes=64)
+        nc.vector.tensor_copy(x2_bytes[:].bitcast(I32), x2_bytes_picked[:].bitcast(I32))
+        place_odd_rows(x2_bytes)
+        x2_codes = sb.tile([P, S], U32, name="x2_codes", align_bytes=64)
+        nc.vector.tensor_copy(x2_codes[:], x_word_table[:].indirect(two_t[:]))
+
+        def round_weight(name, raw):
+            grouped = sb.tile([P, PACK, P, PACK], BF16, name=name + "_bf", tag=name + "_bf", align_bytes=64)
+            dst = grouped[:].rearrange("p t m j -> p m j t")
+            src = raw[:].rearrange("p j (m t) -> p m j t", t=PACK)
+            step = P // CAST_PARTS
+            for m0 in range(0, P, step):
+                nc.vector.tensor_copy(dst[:, m0 : m0 + step], src[:, m0 : m0 + step])
+            return grouped
+
+        def quantise_weight(name, grouped):
+            codes = sb.tile([P, N], U32, name=name + "_codes", align_bytes=64)
+            scale = sb.tile([P, N], U8, name=name + "_bytes", align_bytes=64)
+            nc.vector.quantize_mx(out=codes[:].bitcast(FP8X4), scales=scale[:], in_=grouped[:].rearrange("p t m j -> p (t m j)"))
+            return codes, scale
+
+        h2_win = [sb.tile([P, 2 * S], F32, name="h2_win%d" % t) for t in range(PACK)]
+        h = [sb.tile([P, S], F32, name="h%d" % t) for t in range(PACK)]
+
+        def fetch_pairs(t):
+            acc = psum.tile([P, S], F32, name="h_acc%d" % t)
+            nc.tensor.matmul_mx(out=acc[:], lhsT=d_codes[:, t, :].bitcast(FP8X4), lhsT_scale=plane[:, t * P : (t + 1) * P],
+                                rhs=xq_codes[:].bitcast(FP8X4), rhs_scale=plane[:, H:], start=True, stop=True)
+            if EVAC[t] == "s":
+                nc.scalar.activation(h[t][:], acc[:], ACT.Copy, scale=0.0625)
+            else:
+                nc.vector.tensor_scalar(h[t][:], acc[:], 0.0625, None, ALU.mult)
+            pa = h2_win[t][:, S : S + W]
+            pb = h2_win[t][:, S + W :]
+            nc.scalar.activation(pa, h[t][:].indirect(n1_t[:]), ACT.Copy)
+            if N2_ENG[t] == "s":
+                nc.scalar.activation(pb, h[t][:].indirect(n2_t[:]), ACT.Copy)
+            else:
+                nc.vector.tensor_copy(pb, h[t][:].indirect(n2_t[:]))
+
+        def put_back(t, ra):
+            nc.vector.tensor_tensor(ra[:], h2_win[t][:, S : S + W], h2_win[t][:, S + W :], ALU.max)
+            nc.scalar.activation(h[t][:].indirect(n1_t[:]), ra[:], ACT.Copy)
+
+        for t in range(PACK):
+            fetch_pairs(t)
+        w2_codes, w2_bytes = quantise_weight("w2", round_weight("w2", w2_raw))
+        put_back(0, sb.tile([P, W], F32, name="ra0", tag="w2_bf", align_bytes=64))
+        for t in range(1, PACK):
+            put_back(t, sb.tile([P, W], F32, name="ra%d" % t))
+        w1_codes, w1_bytes = quantise_weight("w1", round_weight("w1", w1_raw))
+        z_bf = sb.tile([P, S, PACK], BF16, name="z_bf", tag="w1_bf", align_bytes=64)
+        for t in range(PACK):
+            nc.vector.tensor_scalar(z_bf[:, :, t], h[t][:], gain[:, t : t + 1], None, ALU.mult)
+
+        z_codes = sb.tile([P, S], U32, name="z_codes", align_bytes=64)
+        z_bytes = sb.tile([P, S], U8, name="z_bytes", align_bytes=64)
+        nc.vector.quantize_mx(out=z_codes[:].bitcast(FP8X4), scales=z_bytes[:], in_=z_bf[:].rearrange("p s t -> p (s t)"))
+
+        out_rows = out.rearrange("(p t) s -> t p s", t=PACK)
+        st_win = [sb.tile([P, 2 * S], F32, name="st_win%d" % t) for t in range(PACK)]
+        for t in range(PACK):
+            cols = slice(t * P, (t + 1) * P)
+            acc = psum.tile([P, S], F32, name="h2_acc%d" % t)
+            nc.tensor.matmul_mx(out=acc[:], lhsT=w2_codes[:, cols].bitcast(FP8X4), lhsT_scale=w2_bytes[:, cols],
+                                rhs=x2_codes[:].bitcast(FP8X4), rhs_scale=x2_bytes[:], start=True, stop=False)
+            nc.tensor.matmul_mx(out=acc[:], lhsT=w1_codes[:, cols].bitcast(FP8X4), lhsT_scale=w1_bytes[:, cols],
+                                rhs=z_codes[:].bitcast(FP8X4), rhs_scale=z_bytes[:], start=False, stop=True)
+            h2 = h2_win[t][:, :S]
+            if EVAC2[t] == "s":
+                nc.scalar.copy(h2, acc[:])
+            else:
+                nc.vector.tensor_copy(h2, acc[:])
+        for t in range(PACK):
+            nc.scalar.activation(st_win[t][:, S:], h2_win[t][:].indirect(n3_t[:]), ACT.Copy)
+            nc.vector.tensor_tensor(st_win[t][:, :S], st_win[t][:, S:], h2_win[t][:, :S], ALU.subtract)
+        for t in range(PACK):
+            gate = sb.tile([P, S], F32, name="gate%d" % t)
+            nc.scalar.activation(gate[:], st_win[t][:].indirect(n4_t[:]), ACT.Sigmoid)
+            res = sb.tile([P, S], F32, name="res%d" % t)
+            nc.vector.tensor_tensor(res[:], gate[:], h2_win[t][:, :S], ALU.mult)
+            nc.sync.dma_start(out_rows[t], res[:])

@@ -18,7 +18,7 @@ ACT = mybir.ActivationFunctionType
 P = 128
 PACK = 4
 N2_ENG = ["s","s","s","s"]
-EVAC = ["s","s","s","s"]
+EVAC = ["v","v","s","s"]
 EVAC2 = ["v","v","v","v"]
 CAST_PARTS = 1
 
@@ -54,6 +54,10 @@ def tile_picked_pqmixfillhopd_none_p_kernel(tc, x_words, x_scales, d_words, d_sc
         two_t = load_list("two_t", two)
         load_scale_rows(nc.sync, d_byte_table, d_scales)
         load_scale_rows(nc.scalar, x_byte_table, x_scales)
+        warm = sb.tile([P, 1], F32, name="warm")
+        nc.gpsimd.memset(warm[:], 0.0)
+        warm_out = sb.tile([P, 1], F32, name="warm_out")
+        nc.scalar.activation(warm_out[:], warm[:], ACT.Sigmoid)
         d_word_table = sb.tile([P, G], U32, name="d_word_table")
         nc.sync.dma_start(d_word_table[:].bitcast(I32), d_words[0].rearrange("p n t -> p (n t)").bitcast(I32))
         x_word_table = sb.tile([P, T], U32, name="x_word_table")
@@ -66,39 +70,36 @@ def tile_picked_pqmixfillhopd_none_p_kernel(tc, x_words, x_scales, d_words, d_sc
         n4_t = load_list("n4_t", n4)
 
         raw_bytes = PACK * N * 4
-        d_bytes_picked = sb.tile([P, H], U8, name="d_bytes_picked", tag="bytes_picked")
+        d_bytes_picked = reuse.tile([P, H], U8, name="d_bytes_picked", offset=raw_bytes - S // 2)
         nc.vector.tensor_copy(d_bytes_picked[:], d_byte_table[:].indirect(k1_t[:]))
-        xq_bytes_picked = reuse.tile([P, S], U8, name="xq_bytes_picked", offset=raw_bytes - S // 2)
+        xq_bytes_picked = sb.tile([P, S], U8, name="xq_bytes_picked")
         nc.vector.tensor_copy(xq_bytes_picked[:], x_byte_table[:].indirect(offs_t[:]))
         plane = sb.tile([P, H + S], U8, name="plane", align_bytes=64)
-        nc.vector.tensor_copy(plane[:, :H].rearrange("p (t m) -> p m t", t=PACK), d_bytes_picked[:].rearrange("p (m t) -> p m t", t=PACK))
         nc.vector.tensor_copy(plane[:, H:].bitcast(I32), xq_bytes_picked[:].bitcast(I32))
+        nc.vector.tensor_copy(plane[:, :H].rearrange("p (t m) -> p m t", t=PACK), d_bytes_picked[:].rearrange("p (m t) -> p m t", t=PACK))
         place_odd_rows(plane)
         w2_raw = reuse.tile([P, PACK, N], F32, name="w2_raw", offset=0)
         nc.sync.dma_start(w2_raw[:], w2.rearrange("(p j) c -> p j c", j=PACK))
-        w1_raw = reuse.tile([P, PACK, N], F32, name="w1_raw", offset=raw_bytes)
+        w1_raw = reuse.tile([P, PACK, N], F32, name="w1_raw", offset=raw_bytes + S)
         nc.sync.dma_start(w1_raw[:], w1.rearrange("(p j) c -> p j c", j=PACK))
 
-        d_words_picked = sb.tile([P, H], U32, name="d_words_picked")
-        nc.vector.tensor_copy(d_words_picked[:], d_word_table[:].indirect(k1_t[:]))
-        d_codes = sb.tile([P, PACK, P], U32, name="d_codes", align_bytes=64)
-        nc.vector.tensor_copy(d_codes[:].bitcast(I32).rearrange("p t m -> p m t"), d_words_picked[:].bitcast(I32).rearrange("p (m t) -> p m t", t=PACK))
-        xq_codes = sb.tile([P, S], U32, name="xq_codes", align_bytes=64)
-        nc.vector.tensor_copy(xq_codes[:], x_word_table[:].indirect(offs_t[:]))
-
-        x2_bytes_picked = sb.tile([P, S], U8, name="x2_bytes_picked", tag="bytes_picked")
+        x2_bytes_picked = reuse.tile([P, S], U8, name="x2_bytes_picked", offset=raw_bytes)
         nc.vector.tensor_copy(x2_bytes_picked[:], x_byte_table[:].indirect(two_t[:]))
         x2_bytes = sb.tile([P, S], U8, name="x2_bytes", align_bytes=64)
         nc.vector.tensor_copy(x2_bytes[:].bitcast(I32), x2_bytes_picked[:].bitcast(I32))
         place_odd_rows(x2_bytes)
-        x2_codes = sb.tile([P, S], U32, name="x2_codes", align_bytes=64)
-        nc.vector.tensor_copy(x2_codes[:], x_word_table[:].indirect(two_t[:]))
+        d_words_picked = sb.tile([P, H], U32, name="d_words_picked")
+        nc.vector.tensor_copy(d_words_picked[:], d_word_table[:].indirect(k1_t[:]))
+        d_codes = sb.tile([P, PACK, P], U32, name="d_codes", tag="d_codes", align_bytes=64)
+        nc.vector.tensor_copy(d_codes[:].bitcast(I32).rearrange("p t m -> p m t"), d_words_picked[:].bitcast(I32).rearrange("p (m t) -> p m t", t=PACK))
+        xq_codes = sb.tile([P, S], U32, name="xq_codes", tag="token_codes", align_bytes=64)
+        nc.vector.tensor_copy(xq_codes[:], x_word_table[:].indirect(offs_t[:]))
 
-        def round_weight(name, raw):
+        def round_weight(name, raw, parts):
             grouped = sb.tile([P, PACK, P, PACK], BF16, name=name + "_bf", tag=name + "_bf", align_bytes=64)
             dst = grouped[:].rearrange("p t m j -> p m j t")
             src = raw[:].rearrange("p j (m t) -> p m j t", t=PACK)
-            step = P // CAST_PARTS
+            step = P // parts
             for m0 in range(0, P, step):
                 nc.vector.tensor_copy(dst[:, m0 : m0 + step], src[:, m0 : m0 + step])
             return grouped
@@ -129,16 +130,19 @@ def tile_picked_pqmixfillhopd_none_p_kernel(tc, x_words, x_scales, d_words, d_sc
                 nc.vector.tensor_copy(pb, h[t][:].indirect(n2_t[:]))
 
         def put_back(t, ra):
-            nc.vector.tensor_tensor(ra[:], h2_win[t][:, S : S + W], h2_win[t][:, S + W :], ALU.max)
-            nc.scalar.activation(h[t][:].indirect(n1_t[:]), ra[:], ACT.Copy)
+            nc.vector.tensor_tensor(ra, h2_win[t][:, S : S + W], h2_win[t][:, S + W :], ALU.max)
+            nc.scalar.activation(h[t][:].indirect(n1_t[:]), ra, ACT.Copy)
 
         for t in range(PACK):
             fetch_pairs(t)
-        w2_codes, w2_bytes = quantise_weight("w2", round_weight("w2", w2_raw))
-        put_back(0, sb.tile([P, W], F32, name="ra0", tag="w2_bf", align_bytes=64))
-        for t in range(1, PACK):
-            put_back(t, sb.tile([P, W], F32, name="ra%d" % t))
-        w1_codes, w1_bytes = quantise_weight("w1", round_weight("w1", w1_raw))
+        x2_codes = sb.tile([P, S], U32, name="x2_codes", tag="token_codes", align_bytes=64)
+        nc.vector.tensor_copy(x2_codes[:], x_word_table[:].indirect(two_t[:]))
+
+        w2_codes, w2_bytes = quantise_weight("w2", round_weight("w2", w2_raw, 1))
+        ra = sb.tile([P, PACK, W], F32, name="ra", tag="w2_bf", align_bytes=64)
+        for t in range(PACK):
+            put_back(t, ra[:, t, :])
+        w1_codes, w1_bytes = quantise_weight("w1", round_weight("w1", w1_raw, 2))
         z_bf = sb.tile([P, S, PACK], BF16, name="z_bf", tag="w1_bf", align_bytes=64)
         for t in range(PACK):
             nc.vector.tensor_scalar(z_bf[:, :, t], h[t][:], gain[:, t : t + 1], None, ALU.mult)

@@ -44,7 +44,7 @@ def tile_picked_pqmixfillhopd_none_p_kernel(tc, x_words, x_scales, d_words, d_sc
             for c in range(2):
                 nc.sync.dma_start(plane[2 + c : P : 32, :].bitcast(I32), plane[16 + c : P : 32, :].bitcast(I32))
 
-        d_byte_table = sb.tile([P, G], U8, name="d_byte_table")
+        d_byte_table = sb.tile([P, G], U8, name="d_byte_table", tag="d_byte_table", align_bytes=64)
         x_byte_table = sb.tile([P, T], U8, name="x_byte_table")
         nc.vector.memset(d_byte_table[:].bitcast(I32), 0)
         nc.gpsimd.memset(x_byte_table[:].bitcast(I32), 0)
@@ -70,24 +70,19 @@ def tile_picked_pqmixfillhopd_none_p_kernel(tc, x_words, x_scales, d_words, d_sc
         n4_t = load_list("n4_t", n4)
 
         raw_bytes = PACK * N * 4
-        d_bytes_picked = reuse.tile([P, H], U8, name="d_bytes_picked", offset=raw_bytes - S // 2)
+        d_bytes_picked = reuse.tile([P, H], U8, name="d_bytes_picked", offset=raw_bytes - H // 2)
         nc.vector.tensor_copy(d_bytes_picked[:], d_byte_table[:].indirect(k1_t[:]))
         xq_bytes_picked = sb.tile([P, S], U8, name="xq_bytes_picked")
         nc.vector.tensor_copy(xq_bytes_picked[:], x_byte_table[:].indirect(offs_t[:]))
-        plane = sb.tile([P, H + S], U8, name="plane", align_bytes=64)
+        plane = sb.tile([P, H + S], U8, name="plane", tag="d_byte_table", align_bytes=64)
         nc.vector.tensor_copy(plane[:, H:].bitcast(I32), xq_bytes_picked[:].bitcast(I32))
         nc.vector.tensor_copy(plane[:, :H].rearrange("p (t m) -> p m t", t=PACK), d_bytes_picked[:].rearrange("p (m t) -> p m t", t=PACK))
         place_odd_rows(plane)
         w2_raw = reuse.tile([P, PACK, N], F32, name="w2_raw", offset=0)
         nc.sync.dma_start(w2_raw[:], w2.rearrange("(p j) c -> p j c", j=PACK))
-        w1_raw = reuse.tile([P, PACK, N], F32, name="w1_raw", offset=raw_bytes + S)
+        w1_raw = reuse.tile([P, PACK, N], F32, name="w1_raw", offset=raw_bytes)
         nc.sync.dma_start(w1_raw[:], w1.rearrange("(p j) c -> p j c", j=PACK))
 
-        x2_bytes_picked = reuse.tile([P, S], U8, name="x2_bytes_picked", offset=raw_bytes)
-        nc.vector.tensor_copy(x2_bytes_picked[:], x_byte_table[:].indirect(two_t[:]))
-        x2_bytes = sb.tile([P, S], U8, name="x2_bytes", align_bytes=64)
-        nc.vector.tensor_copy(x2_bytes[:].bitcast(I32), x2_bytes_picked[:].bitcast(I32))
-        place_odd_rows(x2_bytes)
         d_words_picked = sb.tile([P, H], U32, name="d_words_picked")
         nc.vector.tensor_copy(d_words_picked[:], d_word_table[:].indirect(k1_t[:]))
         d_codes = sb.tile([P, PACK, P], U32, name="d_codes", tag="d_codes", align_bytes=64)
@@ -104,10 +99,10 @@ def tile_picked_pqmixfillhopd_none_p_kernel(tc, x_words, x_scales, d_words, d_sc
                 nc.vector.tensor_copy(dst[:, m0 : m0 + step], src[:, m0 : m0 + step])
             return grouped
 
-        def quantise_weight(name, grouped):
-            codes = sb.tile([P, N], U32, name=name + "_codes", align_bytes=64)
-            scale = sb.tile([P, N], U8, name=name + "_bytes", align_bytes=64)
-            nc.vector.quantize_mx(out=codes[:].bitcast(FP8X4), scales=scale[:], in_=grouped[:].rearrange("p t m j -> p (t m j)"))
+        def quantise_weight(grouped, half, codes):
+            scale = sb.tile([P, N // 2], U8, name="w_bytes", bufs=4, align_bytes=64)
+            nc.vector.quantize_mx(out=codes[:].bitcast(FP8X4), scales=scale[:],
+                                  in_=grouped[:, 2 * half : 2 * half + 2].rearrange("p t m j -> p (t m j)"))
             return codes, scale
 
         h2_win = [sb.tile([P, 2 * S], F32, name="h2_win%d" % t) for t in range(PACK)]
@@ -135,15 +130,24 @@ def tile_picked_pqmixfillhopd_none_p_kernel(tc, x_words, x_scales, d_words, d_sc
 
         for t in range(PACK):
             fetch_pairs(t)
+        x2_bytes_picked = sb.tile([P, S], U8, name="x2_bytes_picked", tag="d_codes", align_bytes=64)
+        nc.vector.tensor_copy(x2_bytes_picked[:], x_byte_table[:].indirect(two_t[:]))
+        x2_bytes = sb.tile([P, S], U8, name="x2_bytes", align_bytes=64)
+        nc.gpsimd.memset(x2_bytes[:].bitcast(I32), 0)
+        for c in range(PACK):
+            nc.sync.dma_start(x2_bytes[c:P:32, :].bitcast(I32), x2_bytes_picked[16 * (c // 2) + c % 2 : P : 32, :].bitcast(I32))
         x2_codes = sb.tile([P, S], U32, name="x2_codes", tag="token_codes", align_bytes=64)
         nc.vector.tensor_copy(x2_codes[:], x_word_table[:].indirect(two_t[:]))
 
-        w2_codes, w2_bytes = quantise_weight("w2", round_weight("w2", w2_raw, 1))
-        ra = sb.tile([P, PACK, W], F32, name="ra", tag="w2_bf", align_bytes=64)
+        w2_bf = round_weight("w2", w2_raw, 1)
+        ra = reuse.tile([P, PACK, W], F32, name="ra", offset=0)
         for t in range(PACK):
             put_back(t, ra[:, t, :])
-        w1_codes, w1_bytes = quantise_weight("w1", round_weight("w1", w1_raw, 2))
-        z_bf = sb.tile([P, S, PACK], BF16, name="z_bf", tag="w1_bf", align_bytes=64)
+        w2_q = [quantise_weight(w2_bf, 0, sb.tile([P, N // 2], U32, name="w2_codes0", align_bytes=64))]
+        w1_bf = round_weight("w1", w1_raw, 1)
+        w1_q = [quantise_weight(w1_bf, 0, sb.tile([P, N // 2], U32, name="w1_codes0", align_bytes=64))]
+        z_at = raw_bytes + H
+        z_bf = reuse.tile([P, S, PACK], BF16, name="z_bf", align_bytes=64, offset=z_at)
         for t in range(PACK):
             nc.vector.tensor_scalar(z_bf[:, :, t], h[t][:], gain[:, t : t + 1], None, ALU.mult)
 
@@ -151,10 +155,15 @@ def tile_picked_pqmixfillhopd_none_p_kernel(tc, x_words, x_scales, d_words, d_sc
         z_bytes = sb.tile([P, S], U8, name="z_bytes", align_bytes=64)
         nc.vector.quantize_mx(out=z_codes[:].bitcast(FP8X4), scales=z_bytes[:], in_=z_bf[:].rearrange("p s t -> p (s t)"))
 
+        w2_q.append(quantise_weight(w2_bf, 1, reuse.tile([P, N // 2], U32, name="w2_codes1", align_bytes=64, offset=z_at)))
+        w1_q.append(quantise_weight(w1_bf, 1, reuse.tile([P, N // 2], U32, name="w1_codes1", align_bytes=64, offset=z_at + 2 * N)))
+
         out_rows = out.rearrange("(p t) s -> t p s", t=PACK)
         st_win = [sb.tile([P, 2 * S], F32, name="st_win%d" % t) for t in range(PACK)]
         for t in range(PACK):
-            cols = slice(t * P, (t + 1) * P)
+            cols = slice(t % 2 * P, (t % 2 + 1) * P)
+            w2_codes, w2_bytes = w2_q[t // 2]
+            w1_codes, w1_bytes = w1_q[t // 2]
             acc = psum.tile([P, S], F32, name="h2_acc%d" % t)
             nc.tensor.matmul_mx(out=acc[:], lhsT=w2_codes[:, cols].bitcast(FP8X4), lhsT_scale=w2_bytes[:, cols],
                                 rhs=x2_codes[:].bitcast(FP8X4), rhs_scale=x2_bytes[:], start=True, stop=False)
@@ -170,7 +179,11 @@ def tile_picked_pqmixfillhopd_none_p_kernel(tc, x_words, x_scales, d_words, d_sc
             nc.vector.tensor_tensor(st_win[t][:, :S], st_win[t][:, S:], h2_win[t][:, :S], ALU.subtract)
         for t in range(PACK):
             gate = sb.tile([P, S], F32, name="gate%d" % t)
-            nc.scalar.activation(gate[:], st_win[t][:].indirect(n4_t[:]), ACT.Sigmoid)
             res = sb.tile([P, S], F32, name="res%d" % t)
-            nc.vector.tensor_tensor(res[:], gate[:], h2_win[t][:, :S], ALU.mult)
-            nc.sync.dma_start(out_rows[t], res[:])
+            pieces = 2 if t == PACK - 1 else 1
+            for u in range(pieces):
+                cols = slice(u * S // pieces, (u + 1) * S // pieces)
+                entries = slice(u * S // pieces // 16, (u + 1) * S // pieces // 16)
+                nc.scalar.activation(gate[:, cols], st_win[t][:].indirect(n4_t[:, entries]), ACT.Sigmoid)
+                nc.vector.tensor_tensor(res[:, cols], gate[:, cols], h2_win[t][:, cols], ALU.mult)
+                nc.sync.dma_start(out_rows[t][:, cols], res[:, cols])

@@ -18,7 +18,7 @@ ACT = mybir.ActivationFunctionType
 P = 128
 PACK = 4
 N2_ENG = ["s","s","s","s"]
-EVAC = ["v","v","s","s"]
+EVAC = ["v","v","v","v"]
 EVAC2 = ["v","v","v","v"]
 CAST_PARTS = 1
 
@@ -64,29 +64,41 @@ def tile_picked_pqmixfillhopd_none_p_kernel(tc, x_words, x_scales, d_words, d_sc
         nc.sync.dma_start(x_word_table[:].bitcast(I32), x_words[0].rearrange("p n t -> p (n t)").bitcast(I32))
         n1_t = load_list("n1_t", n1)
         n2_t = load_list("n2_t", n2)
-        gain = sb.tile([P, PACK], F32, name="gain")
-        nc.gpsimd.dma_start(gain[:], gn.rearrange("(p t) o -> p (t o)", t=PACK))
         n3_t = load_list("n3_t", n3)
         n4_t = load_list("n4_t", n4)
 
         raw_bytes = PACK * N * 4
-        d_bytes_picked = reuse.tile([P, H], U8, name="d_bytes_picked", offset=raw_bytes - H // 2)
+        d_bytes_picked = reuse.tile([P, H], U8, name="d_bytes_picked", offset=raw_bytes - S // 2)
         nc.vector.tensor_copy(d_bytes_picked[:], d_byte_table[:].indirect(k1_t[:]))
         xq_bytes_picked = sb.tile([P, S], U8, name="xq_bytes_picked")
         nc.vector.tensor_copy(xq_bytes_picked[:], x_byte_table[:].indirect(offs_t[:]))
         plane = sb.tile([P, H + S], U8, name="plane", tag="d_byte_table", align_bytes=64)
         nc.vector.tensor_copy(plane[:, H:].bitcast(I32), xq_bytes_picked[:].bitcast(I32))
-        nc.vector.tensor_copy(plane[:, :H].rearrange("p (t m) -> p m t", t=PACK), d_bytes_picked[:].rearrange("p (m t) -> p m t", t=PACK))
+        nc.vector.tensor_copy(plane[:, :H].bitcast(I32).rearrange("p (t a) -> p a t", t=PACK), d_bytes_picked[:].bitcast(I32).rearrange("p (a t) -> p a t", t=PACK))
         place_odd_rows(plane)
         w2_raw = reuse.tile([P, PACK, N], F32, name="w2_raw", offset=0)
         nc.sync.dma_start(w2_raw[:], w2.rearrange("(p j) c -> p j c", j=PACK))
-        w1_raw = reuse.tile([P, PACK, N], F32, name="w1_raw", offset=raw_bytes)
-        nc.sync.dma_start(w1_raw[:], w1.rearrange("(p j) c -> p j c", j=PACK))
+        w1_raw = reuse.tile([P, PACK, N], F32, name="w1_raw", offset=raw_bytes + S + 32)
+        w1_rows = w1.rearrange("(a j r) c -> r a j c", j=PACK, r=PACK)
+        for r in range(PACK):
+            nc.sync.dma_start(w1_raw[r:P:PACK], w1_rows[r])
+        gain = reuse.tile([P, PACK], F32, name="gain", offset=raw_bytes + S)
+        gain_rows = gn.rearrange("(a t r) o -> r a (t o)", t=PACK, r=PACK)
+        with nc.allow_non_contiguous_dma(reason="four gains a partition, four rows apart"):
+            for r in range(PACK):
+                nc.sync.dma_start(gain[r:P:PACK, :], gain_rows[r])
+
+        x2_bytes_picked = reuse.tile([P, S], U8, name="x2_bytes_picked", offset=raw_bytes)
+        nc.vector.tensor_copy(x2_bytes_picked[:], x_byte_table[:].indirect(two_t[:]))
+        x2_bytes = sb.tile([P, S], U8, name="x2_bytes", align_bytes=64)
+        nc.gpsimd.memset(x2_bytes[:].bitcast(I32), 0)
+        for c in range(PACK):
+            nc.sync.dma_start(x2_bytes[c:P:32, :].bitcast(I32), x2_bytes_picked[16 * (c // 2) + c % 2 : P : 32, :].bitcast(I32))
 
         d_words_picked = sb.tile([P, H], U32, name="d_words_picked")
         nc.vector.tensor_copy(d_words_picked[:], d_word_table[:].indirect(k1_t[:]))
-        d_codes = sb.tile([P, PACK, P], U32, name="d_codes", tag="d_codes", align_bytes=64)
-        nc.vector.tensor_copy(d_codes[:].bitcast(I32).rearrange("p t m -> p m t"), d_words_picked[:].bitcast(I32).rearrange("p (m t) -> p m t", t=PACK))
+        d_codes = sb.tile([P, PACK, P], U32, name="d_codes", align_bytes=64)
+        nc.vector.tensor_copy(d_codes[:].bitcast(I32).rearrange("p t (a r) -> p a t r", r=PACK), d_words_picked[:].bitcast(I32).rearrange("p (a t r) -> p a t r", t=PACK, r=PACK))
         xq_codes = sb.tile([P, S], U32, name="xq_codes", tag="token_codes", align_bytes=64)
         nc.vector.tensor_copy(xq_codes[:], x_word_table[:].indirect(offs_t[:]))
 
@@ -130,12 +142,6 @@ def tile_picked_pqmixfillhopd_none_p_kernel(tc, x_words, x_scales, d_words, d_sc
 
         for t in range(PACK):
             fetch_pairs(t)
-        x2_bytes_picked = sb.tile([P, S], U8, name="x2_bytes_picked", tag="d_codes", align_bytes=64)
-        nc.vector.tensor_copy(x2_bytes_picked[:], x_byte_table[:].indirect(two_t[:]))
-        x2_bytes = sb.tile([P, S], U8, name="x2_bytes", align_bytes=64)
-        nc.gpsimd.memset(x2_bytes[:].bitcast(I32), 0)
-        for c in range(PACK):
-            nc.sync.dma_start(x2_bytes[c:P:32, :].bitcast(I32), x2_bytes_picked[16 * (c // 2) + c % 2 : P : 32, :].bitcast(I32))
         x2_codes = sb.tile([P, S], U32, name="x2_codes", tag="token_codes", align_bytes=64)
         nc.vector.tensor_copy(x2_codes[:], x_word_table[:].indirect(two_t[:]))
 

from contextlib import ExitStack

import concourse.mybir as mybir

K, T, S, N, G, H, W = 512, 1024, 256, 512, 2048, 512, 128
FLOPS = 2 * K * H * S + 2 * H * N * S + 2 * K * N * S

F32 = mybir.dt.float32
BF16 = mybir.dt.bfloat16
I32 = mybir.dt.int32
U32 = mybir.dt.uint32
U16 = mybir.dt.uint16
U8 = mybir.dt.uint8
FP8X4 = mybir.dt.float8_e4m3fn_x4
ALU = mybir.AluOpType
ACT = mybir.ActivationFunctionType

P = 128
PACK = 4
N2_ENG = ["s","s","s","s"]
EVAC = ["v","v","v","v"]
EVAC2 = ["v","v","v","v"]
CAST_PARTS = 1


def tile_picked_pqmixfillhopd_none_p_kernel(tc, x_words, x_scales, d_words, d_scales, gn, w1, w2, offs, k1, n1, n2, two, n3, n4, out):
    nc = tc.nc
    with ExitStack() as ctx:
        sb = ctx.enter_context(tc.tile_pool(name="sb", bufs=1))
        reuse = ctx.enter_context(tc.tile_pool(name="reuse", bufs=1))
        psum = ctx.enter_context(tc.psum_pool(name="psum", bufs=1))

        def load_list(name, src):
            lst = sb.tile(list(src.shape), U16, name=name)
            nc.sync.dma_start(lst[:], src)
            return lst

        def load_scale_rows(queue, table, scales):
            rows = scales[0].bitcast(I32).rearrange("(r c) n -> c r n", c=2)
            for c in range(2):
                queue.dma_start(table[c:P:16, :].bitcast(I32), rows[c])

        def place_odd_rows(plane):
            for c in range(2):
                nc.sync.dma_start(plane[2 + c : P : 32, :].bitcast(I32), plane[16 + c : P : 32, :].bitcast(I32))

        d_byte_table = sb.tile([P, G], U8, name="d_byte_table", tag="d_byte_table", align_bytes=64)
        x_byte_table = sb.tile([P, T], U8, name="x_byte_table")
        nc.vector.memset(d_byte_table[:].bitcast(I32), 0)
        nc.gpsimd.memset(x_byte_table[:].bitcast(I32), 0)

        k1_t = load_list("k1_t", k1)
        offs_t = load_list("offs_t", offs)
        two_t = load_list("two_t", two)
        load_scale_rows(nc.sync, d_byte_table, d_scales)
        load_scale_rows(nc.scalar, x_byte_table, x_scales)
        warm = sb.tile([P, 1], F32, name="warm")
        nc.gpsimd.memset(warm[:], 0.0)
        warm_out = sb.tile([P, 1], F32, name="warm_out")
        nc.scalar.activation(warm_out[:], warm[:], ACT.Sigmoid)
        d_word_table = sb.tile([P, G], U32, name="d_word_table")
        nc.sync.dma_start(d_word_table[:].bitcast(I32), d_words[0].rearrange("p n t -> p (n t)").bitcast(I32))
        x_word_table = sb.tile([P, T], U32, name="x_word_table")
        nc.sync.dma_start(x_word_table[:].bitcast(I32), x_words[0].rearrange("p n t -> p (n t)").bitcast(I32))
        n1_t = load_list("n1_t", n1)
        n2_t = load_list("n2_t", n2)
        n3_t = load_list("n3_t", n3)
        n4_t = load_list("n4_t", n4)

        raw_bytes = PACK * N * 4
        d_bytes_picked = reuse.tile([P, H], U8, name="d_bytes_picked", offset=raw_bytes - S // 2)
        nc.vector.tensor_copy(d_bytes_picked[:], d_byte_table[:].indirect(k1_t[:]))
        xq_bytes_picked = sb.tile([P, S], U8, name="xq_bytes_picked")
        nc.vector.tensor_copy(xq_bytes_picked[:], x_byte_table[:].indirect(offs_t[:]))
        plane = sb.tile([P, H + S], U8, name="plane", tag="d_byte_table", align_bytes=64)
        nc.vector.tensor_copy(plane[:, H:].bitcast(I32), xq_bytes_picked[:].bitcast(I32))
        nc.vector.tensor_copy(plane[:, :H].bitcast(I32).rearrange("p (t a) -> p a t", t=PACK), d_bytes_picked[:].bitcast(I32).rearrange("p (a t) -> p a t", t=PACK))
        place_odd_rows(plane)
        w2_raw = reuse.tile([P, PACK, N], F32, name="w2_raw", offset=0)
        nc.sync.dma_start(w2_raw[:], w2.rearrange("(p j) c -> p j c", j=PACK))
        w1_raw = reuse.tile([P, PACK, N], F32, name="w1_raw", offset=raw_bytes + S + 32)
        w1_rows = w1.rearrange("(a j r) c -> r a j c", j=PACK, r=PACK)
        for r in range(PACK):
            nc.sync.dma_start(w1_raw[r:P:PACK], w1_rows[r])
        gain = reuse.tile([P, PACK], F32, name="gain", offset=raw_bytes + S)
        gain_rows = gn.rearrange("(a t r) o -> r a (t o)", t=PACK, r=PACK)
        with nc.allow_non_contiguous_dma(reason="four gains a partition, four rows apart"):
            for r in range(PACK):
                nc.sync.dma_start(gain[r:P:PACK, :], gain_rows[r])

        x2_bytes_picked = reuse.tile([P, S], U8, name="x2_bytes_picked", offset=raw_bytes)
        nc.vector.tensor_copy(x2_bytes_picked[:], x_byte_table[:].indirect(two_t[:]))
        x2_bytes = sb.tile([P, S], U8, name="x2_bytes", align_bytes=64)
        nc.gpsimd.memset(x2_bytes[:].bitcast(I32), 0)
        for c in range(PACK):
            nc.sync.dma_start(x2_bytes[c:P:32, :].bitcast(I32), x2_bytes_picked[16 * (c // 2) + c % 2 : P : 32, :].bitcast(I32))

        d_words_picked = sb.tile([P, H], U32, name="d_words_picked")
        nc.vector.tensor_copy(d_words_picked[:], d_word_table[:].indirect(k1_t[:]))
        d_codes = sb.tile([P, PACK, P], U32, name="d_codes", align_bytes=64)
        nc.vector.tensor_copy(d_codes[:].bitcast(I32).rearrange("p t (a r) -> p a t r", r=PACK), d_words_picked[:].bitcast(I32).rearrange("p (a t r) -> p a t r", t=PACK, r=PACK))
        xq_codes = sb.tile([P, S], U32, name="xq_codes", tag="token_codes", align_bytes=64)
        nc.vector.tensor_copy(xq_codes[:], x_word_table[:].indirect(offs_t[:]))

        def round_weight(name, raw, parts):
            grouped = sb.tile([P, PACK, P, PACK], BF16, name=name + "_bf", tag=name + "_bf", align_bytes=64)
            dst = grouped[:].rearrange("p t m j -> p m j t")
            src = raw[:].rearrange("p j (m t) -> p m j t", t=PACK)
            step = P // parts
            for m0 in range(0, P, step):
                nc.vector.tensor_copy(dst[:, m0 : m0 + step], src[:, m0 : m0 + step])
            return grouped

        def quantise_weight(grouped, half, codes):
            scale = sb.tile([P, N // 2], U8, name="w_bytes", bufs=4, align_bytes=64)
            nc.vector.quantize_mx(out=codes[:].bitcast(FP8X4), scales=scale[:],
                                  in_=grouped[:, 2 * half : 2 * half + 2].rearrange("p t m j -> p (t m j)"))
            return codes, scale

        h2_win = [sb.tile([P, 2 * S], F32, name="h2_win%d" % t) for t in range(PACK)]
        h = [sb.tile([P, S], F32, name="h%d" % t) for t in range(PACK)]

        def fetch_pairs(t):
            acc = psum.tile([P, S], F32, name="h_acc%d" % t)
            nc.tensor.matmul_mx(out=acc[:], lhsT=d_codes[:, t, :].bitcast(FP8X4), lhsT_scale=plane[:, t * P : (t + 1) * P],
                                rhs=xq_codes[:].bitcast(FP8X4), rhs_scale=plane[:, H:], start=True, stop=True)
            if EVAC[t] == "s":
                nc.scalar.activation(h[t][:], acc[:], ACT.Copy, scale=0.0625)
            else:
                nc.vector.tensor_scalar(h[t][:], acc[:], 0.0625, None, ALU.mult)
            pa = h2_win[t][:, S : S + W]
            pb = h2_win[t][:, S + W :]
            nc.scalar.activation(pa, h[t][:].indirect(n1_t[:]), ACT.Copy)
            if N2_ENG[t] == "s":
                nc.scalar.activation(pb, h[t][:].indirect(n2_t[:]), ACT.Copy)
            else:
                nc.vector.tensor_copy(pb, h[t][:].indirect(n2_t[:]))

        def put_back(t, ra):
            nc.vector.tensor_tensor(ra, h2_win[t][:, S : S + W], h2_win[t][:, S + W :], ALU.max)
            nc.scalar.activation(h[t][:].indirect(n1_t[:]), ra, ACT.Copy)

        for t in range(PACK):
            fetch_pairs(t)
        x2_codes = sb.tile([P, S], U32, name="x2_codes", tag="token_codes", align_bytes=64)
        nc.vector.tensor_copy(x2_codes[:], x_word_table[:].indirect(two_t[:]))

        w2_bf = round_weight("w2", w2_raw, 1)
        ra = reuse.tile([P, PACK, W], F32, name="ra", offset=0)
        for t in range(PACK):
            put_back(t, ra[:, t, :])
        w2_q = [quantise_weight(w2_bf, 0, sb.tile([P, N // 2], U32, name="w2_codes0", align_bytes=64))]
        w1_bf = round_weight("w1", w1_raw, 1)
        w1_q = [quantise_weight(w1_bf, 0, sb.tile([P, N // 2], U32, name="w1_codes0", align_bytes=64))]
        z_at = raw_bytes + H
        z_bf = reuse.tile([P, S, PACK], BF16, name="z_bf", align_bytes=64, offset=z_at)
        for t in range(PACK):
            nc.vector.tensor_scalar(z_bf[:, :, t], h[t][:], gain[:, t : t + 1], None, ALU.mult)

        z_codes = sb.tile([P, S], U32, name="z_codes", align_bytes=64)
        z_bytes = sb.tile([P, S], U8, name="z_bytes", align_bytes=64)
        nc.vector.quantize_mx(out=z_codes[:].bitcast(FP8X4), scales=z_bytes[:], in_=z_bf[:].rearrange("p s t -> p (s t)"))

        w2_q.append(quantise_weight(w2_bf, 1, reuse.tile([P, N // 2], U32, name="w2_codes1", align_bytes=64, offset=z_at)))
        w1_q.append(quantise_weight(w1_bf, 1, reuse.tile([P, N // 2], U32, name="w1_codes1", align_bytes=64, offset=z_at + 2 * N)))

        out_rows = out.rearrange("(p t) s -> t p s", t=PACK)
        st_win = [sb.tile([P, 2 * S], F32, name="st_win%d" % t) for t in range(PACK)]
        for t in range(PACK):
            cols = slice(t % 2 * P, (t % 2 + 1) * P)
            w2_codes, w2_bytes = w2_q[t // 2]
            w1_codes, w1_bytes = w1_q[t // 2]
            acc = psum.tile([P, S], F32, name="h2_acc%d" % t)
            nc.tensor.matmul_mx(out=acc[:], lhsT=w2_codes[:, cols].bitcast(FP8X4), lhsT_scale=w2_bytes[:, cols],
                                rhs=x2_codes[:].bitcast(FP8X4), rhs_scale=x2_bytes[:], start=True, stop=False)
            nc.tensor.matmul_mx(out=acc[:], lhsT=w1_codes[:, cols].bitcast(FP8X4), lhsT_scale=w1_bytes[:, cols],
                                rhs=z_codes[:].bitcast(FP8X4), rhs_scale=z_bytes[:], start=False, stop=True)
            h2 = h2_win[t][:, :S]
            if EVAC2[t] == "s":
                nc.scalar.copy(h2, acc[:])
            else:
                nc.vector.tensor_copy(h2, acc[:])
        for t in range(PACK):
            nc.scalar.activation(st_win[t][:, S:], h2_win[t][:].indirect(n3_t[:]), ACT.Copy)
            nc.vector.tensor_tensor(st_win[t][:, :S], st_win[t][:, S:], h2_win[t][:, :S], ALU.subtract)
        for t in range(PACK):
            gate = sb.tile([P, S], F32, name="gate%d" % t)
            res = sb.tile([P, S], F32, name="res%d" % t)
            pieces = 2 if t == PACK - 1 else 1
            for u in range(pieces):
                cols = slice(u * S // pieces, (u + 1) * S // pieces)
                entries = slice(u * S // pieces // 16, (u + 1) * S // pieces // 16)
                nc.scalar.activation(gate[:, cols], st_win[t][:].indirect(n4_t[:, entries]), ACT.Sigmoid)
                nc.vector.tensor_tensor(res[:, cols], gate[:, cols], h2_win[t][:, cols], ALU.mult)
                nc.sync.dma_start(out_rows[t][:, cols], res[:, cols])
